import numpy as np
import ml_dtypes


def mxq(x, axis, fmt="e4m3"):
    dtype, down = {"e4m3": (ml_dtypes.float8_e4m3fn, 7), "e5m2": (ml_dtypes.float8_e5m2, 14)}[fmt]
    v = np.moveaxis(np.asarray(x, np.float32).astype(ml_dtypes.bfloat16).astype(np.float64), axis, -1)
    blocks = v.reshape(v.shape[:-1] + (-1, 32))
    amax = np.abs(blocks).max(-1, keepdims=True)
    byte = np.maximum(np.where(amax > 0, np.frexp(amax)[1] - 1 + 127, 0) - down, 1)
    scale = np.exp2(byte - 127.0)
    codes = (blocks / scale).astype(np.float32).astype(dtype).astype(np.float64)
    return np.moveaxis((codes * scale).reshape(v.shape), -1, axis)


WIDE = False


def mx_kscale(k):
    if not WIDE:
        return np.ones(k)
    levels = np.array([10, -10, 5, -5, 0])
    if k % 512:
        return np.exp2(np.random.permutation(np.resize(levels, k // 32))).repeat(32)
    a = np.empty((k // 512, 16))
    for p in range(k // 512):
        a[p, :8] = np.random.permutation(np.resize(levels, 8))
        for g in range(8):
            far = levels[np.abs(levels - a[p, g]) >= 10]
            a[p, g + 8] = far[np.random.randint(len(far))]
    return np.exp2(a.ravel()).repeat(32)


def f64(x):
    return np.asarray(x).astype(np.float64)


def striped(idx):
    return np.tile(np.asarray(idx).reshape(-1, 16).T, (8, 1)).astype(np.uint16)


def unstriped(offs):
    return offs[:16].T.reshape(-1).astype(np.int64)


E2M1 = np.array([0.0, 0.5, 1.0, 1.5, 2.0, 3.0, 4.0, 6.0, -0.0, -0.5, -1.0, -1.5, -2.0, -3.0, -4.0, -6.0])


def pack_weight(w, fmt):
    k, n = w.shape
    w = f64(np.asarray(w, np.float32).astype(ml_dtypes.bfloat16)).reshape(k // 32, 32, n)
    amax = np.abs(w).max(1)
    if fmt == "e4m3":
        byte = np.frexp(amax)[1] - 1 + 127 - 7
    else:
        mant, ex = np.frexp(amax / 6.0)
        byte = np.where(mant > 0.5, ex, ex - 1) + 127
    byte = np.clip(np.where(amax > 0, byte, 1), 1, 254)
    scaled = (w * np.exp2(127.0 - byte)[:, None, :]).reshape(k, n).astype(np.float32)
    by_word = np.ascontiguousarray(scaled.reshape(k // 512, 128, 4, n).transpose(0, 1, 3, 2))
    if fmt == "e4m3":
        words = by_word.astype(ml_dtypes.float8_e4m3fn).view(np.uint8)
    else:
        c = by_word.astype(ml_dtypes.float4_e2m1fn).view(np.uint8) & 0xF
        words = (c[..., 0::2] | (c[..., 1::2] << 4)).reshape(k // 512, 128, 2 * n)
    return np.ascontiguousarray(words), np.ascontiguousarray(byte.astype(np.uint8).reshape(k // 512, 16, n))


def unpack_weight(words, scales, fmt):
    g, _, n = scales.shape
    words = np.ascontiguousarray(words).reshape(g, 128, n, -1)
    if fmt == "e4m3":
        vals = words.view(ml_dtypes.float8_e4m3fn).astype(np.float64)
    else:
        nib = np.empty((g, 128, n, 4), np.uint8)
        nib[..., 0::2] = words & 0xF
        nib[..., 1::2] = words >> 4
        vals = E2M1[nib]
    vals = vals * np.repeat(np.exp2(scales.astype(np.float64) - 127.0), 8, axis=1)[..., None]
    return vals.transpose(0, 1, 3, 2).reshape(g * 512, n)


def bf(x):
    return np.asarray(x, np.float32).astype(ml_dtypes.bfloat16)


def planes(Y):
    r, m = Y.shape
    b = f64(bf(Y)).reshape(r // 32, 32, m)
    amax = np.abs(b).max(1)
    byte = np.clip(np.where(amax > 0, np.frexp(amax)[1] - 1 + 127 - 7, 1), 1, 254)
    codes = (b * np.exp2(127.0 - byte)[:, None, :]).reshape(r, m).astype(np.float32).astype(ml_dtypes.float8_e4m3fn).view(np.uint8)
    words = codes.reshape(r // 512, 128, 4, m).transpose(0, 1, 3, 2)
    return np.ascontiguousarray(words), np.ascontiguousarray(byte.astype(np.uint8).reshape(r // 512, 16, m))


D, K, T, I, Q = 512, 512, 2048, 512, 256


def setup_inputs():
    n = np.random.standard_normal
    idx = np.random.permutation(T)[:I]
    fd = mx_kscale(D)
    candp = pack_weight(n((D, T)) / fd[:, None], "e2m1")
    return {
        "cand_words": candp[0],
        "cand_scales": candp[1],
        "theta": (n((D, Q)) * 1 / np.sqrt(D) * fd[:, None]).astype(np.float32),
        "inv": (n((D, K)) * 1.5 / np.sqrt(D) * fd[:, None]).astype(np.float32),
        "crow": (n((K, T))).astype(np.float32),
        "bold": (np.random.uniform(1.0, 3.0, (1, Q))).astype(np.float32),
        "offs": striped(idx),
    }


def reference(cand_words, cand_scales, theta, inv, crow, bold, offs):
    idx = unstriped(offs)
    candu = unpack_weight(cand_words, cand_scales, "e2m1")
    candidxg = candu[:, idx]
    thetaq = mxq(f64(theta), 0, "e4m3")
    a = candidxg.T @ thetaq
    invq = mxq(f64(inv), 0, "e4m3")
    z = candidxg.T @ invq
    cr = f64(crow)[:, idx].T
    qf = np.sqrt(np.abs(np.sum(z * cr, axis=1, keepdims=True)) / 512.0 + 0.01)
    y = a + qf * f64(bold)
    words, scales = planes(y)
    return y, words, scales

@@ -1,0 +1,156 @@
+from contextlib import ExitStack
+
+import concourse.mybir as mybir
+from concourse.masks import make_identity
+
+D, K, T, I, Q = 512, 512, 2048, 512, 256
+FLOPS = 2 * D * I * (K + Q)
+
+P = 128
+PACK = 4
+SHARE = 288
+SHARE_FUSED = 256
+F32 = mybir.dt.float32
+BF16 = mybir.dt.bfloat16
+I32 = mybir.dt.int32
+U32 = mybir.dt.uint32
+U16 = mybir.dt.uint16
+U8 = mybir.dt.uint8
+FP8X4 = mybir.dt.float8_e4m3fn_x4
+FP4X4 = mybir.dt.float4_e2m1fn_x4
+ALU = mybir.AluOpType
+ACT = mybir.ActivationFunctionType
+
+
+def interleave(copy, dst, src):
+    copy(dst.rearrange("p (c i) j -> p c j i", i=4), src.rearrange("p j (c i) -> p c j i", i=4))
+
+
+def tile_attend_confidencebounds_pl_kernel(tc, cand_words, cand_scales, theta, inv, crow, bold, offs, out_0, out_1, out_2):
+    nc = tc.nc
+    chunks = K // P
+    last = chunks - 1
+    with ExitStack() as ctx:
+        sb = ctx.enter_context(tc.tile_pool(name="sb", bufs=1))
+        ps = ctx.enter_context(tc.psum_pool(name="ps", bufs=1))
+
+        offsets = sb.tile([P, I // 16], U16, name="offsets")
+        words = sb.tile([P, T], U16, name="words", align_bytes=64)
+        scales = sb.tile([P, T], U8, name="scales", align_bytes=64)
+        inv_raw = sb.tile([P, PACK, K], F32, name="inv_raw")
+        theta_raw = sb.tile([P, PACK, Q], F32, name="theta_raw")
+        bold_col = sb.tile([P, 2], F32, name="bold_col")
+        crow_sb = [sb.tile([P, T], F32, name=f"crow{c}") for c in range(chunks)]
+        ident = sb.tile([P, P], F32, name="ident")
+
+        nc.vector.memset(scales[:].bitcast(I32), 0)
+        nc.sync.dma_start(offsets[:], offs)
+        nc.sync.dma_start(words[:].bitcast(I32), cand_words[0].bitcast(I32))
+        for g in range(4):
+            nc.scalar.dma_start(scales[32 * g : 32 * g + 4, :].bitcast(I32), cand_scales[0, 4 * g : 4 * g + 4, :].bitcast(I32))
+        nc.sync.dma_start(inv_raw[:], inv.rearrange("(p j) k -> p j k", j=PACK))
+        nc.scalar.dma_start(bold_col[:], bold.rearrange("o (p j) -> p (o j)", j=2))
+        for c in range(last):
+            nc.sync.dma_start(crow_sb[c][:], crow[c * P : (c + 1) * P, :])
+        nc.sync.dma_start(theta_raw[:], theta.rearrange("(p j) q -> p j q", j=PACK))
+        nc.sync.dma_start(crow_sb[last][:], crow[last * P :, :])
+        make_identity(nc, ident[:])
+
+        cw = sb.tile([P, I], U16, name="cw", align_bytes=64)
+        cs = sb.tile([P, I], U8, name="cs", align_bytes=64)
+        nc.vector.tensor_copy(cw[:], words[:].indirect(offsets[:]))
+        nc.vector.tensor_copy(cs[:], scales[:].indirect(offsets[:]))
+
+        bold_ps = ps.tile([P, 512], F32, name="bold_ps", tag="spare")
+        for j in range(2):
+            nc.tensor.transpose(bold_ps[:, j * P : (j + 1) * P], bold_col[:, j : j + 1].to_broadcast([P, P]), ident[:])
+        bold_sb = sb.tile([P, Q], F32, name="bold_sb")
+        nc.scalar.copy(bold_sb[:].rearrange("p (n j) -> p n j", j=2), bold_ps[:, 0:Q].rearrange("p (j n) -> p n j", j=2))
+
+        inv_bf = []
+        for c in range(chunks):
+            b = sb.tile([P, P, PACK], BF16, name=f"inv_bf{c}", align_bytes=64)
+            interleave(nc.vector.tensor_copy if c < 2 else nc.scalar.copy, b[:], inv_raw[:, :, c * P : (c + 1) * P])
+            inv_bf.append(b)
+
+        dw = sb.tile([P, PACK, P], U16, name="dw", align_bytes=64)
+        ds = sb.tile([P, PACK, P], U8, name="ds", align_bytes=64)
+
+        z_sb = []
+        for c in range(chunks):
+            iw = sb.tile([P, P], U32, name=f"inv_w{c}", align_bytes=64)
+            isc = sb.tile([P, P], U8, name=f"inv_s{c}", align_bytes=64)
+            nc.vector.quantize_mx(iw[:].bitcast(FP8X4), isc[:], inv_bf[c][:].rearrange("p n j -> p (n j)"))
+            z_ps = ps.tile([P, I], F32, name=f"z_ps{c}", tag=f"bank{c}")
+            if c < last:
+                nc.tensor.matmul_mx(z_ps[:], lhsT=iw[:].bitcast(FP8X4), lhsT_scale=isc[:], rhs=cw[:].bitcast(FP4X4), rhs_scale=cs[:], start=True, stop=True)
+            else:
+                nc.vector.tensor_copy(dw[:], cw[:].rearrange("p (s t) -> p t s", t=PACK))
+                nc.vector.tensor_copy(ds[:], cs[:].rearrange("p (s t) -> p t s", t=PACK))
+                for t in range(PACK):
+                    nc.tensor.matmul_mx(z_ps[:, t * P : (t + 1) * P], lhsT=dw[:, t, :].bitcast(FP4X4), lhsT_scale=ds[:, t, :], rhs=iw[:].bitcast(FP8X4), rhs_scale=isc[:], start=True, stop=True)
+            z = sb.tile([P, I], F32, name=f"z_sb{c}")
+            nc.scalar.copy(z[:], z_ps[:])
+            z_sb.append(z)
+
+        acc = ps.tile([P, PACK, P], F32, name="acc")
+        for c in range(last):
+            prod = sb.tile([P, I], F32, name=f"prod{c}")
+            if c < last - 1 or SHARE_FUSED == I:
+                nc.vector.tensor_tensor(prod[:], crow_sb[c][:].indirect(offsets[:]), z_sb[c][:], ALU.mult)
+            else:
+                n = SHARE_FUSED
+                rest = sb.tile([P, I - n], F32, name="rest")
+                nc.scalar.activation(rest[:], crow_sb[c][:].indirect(offsets[:, n // 16 :]), ACT.Copy)
+                nc.vector.tensor_tensor(prod[:, :n], crow_sb[c][:].indirect(offsets[:, : n // 16]), z_sb[c][:, :n], ALU.mult)
+                nc.vector.tensor_tensor(prod[:, n:], rest[:], z_sb[c][:, n:], ALU.mult)
+            dealt = prod[:].rearrange("p (s t) -> p t s", t=PACK)
+            for t in range(PACK):
+                nc.tensor.matmul(acc[:, t, :], lhsT=dealt[:, t, :], rhs=ident[:], is_transpose=True, start=(c == 0 and t == 0), stop=(c == last - 1 and t == PACK - 1))
+
+        theta_bf = sb.tile([P, Q, PACK], BF16, name="theta_bf", align_bytes=64)
+        interleave(nc.scalar.copy, theta_bf[:], theta_raw[:])
+        tw = sb.tile([P, Q], U32, name="theta_w", align_bytes=64)
+        tsc = sb.tile([P, Q], U8, name="theta_s", align_bytes=64)
+        nc.vector.quantize_mx(tw[:].bitcast(FP8X4), tsc[:], theta_bf[:].rearrange("p n j -> p (n j)"))
+        a_ps = [ps.tile([P, 2, Q], F32, name=f"a_ps{h}") for h in range(2)]
+        for t in range(PACK):
+            nc.tensor.matmul_mx(a_ps[t // 2][:, t % 2, :], lhsT=dw[:, t, :].bitcast(FP4X4), lhsT_scale=ds[:, t, :], rhs=tw[:].bitcast(FP8X4), rhs_scale=tsc[:], start=True, stop=True)
+
+        picked = sb.tile([P, I], F32, name="picked")
+        nc.vector.tensor_copy(picked[:, :SHARE], crow_sb[last][:].indirect(offsets[:, : SHARE // 16]))
+        nc.scalar.activation(picked[:, SHARE:], crow_sb[last][:].indirect(offsets[:, SHARE // 16 :]), ACT.Copy)
+        part = sb.tile([P, PACK], F32, name="part")
+        nc.vector.tensor_reduce(part[:], acc[:], mybir.AxisListType.X, ALU.add)
+        dealt = picked[:].rearrange("p (s t) -> p t s", t=PACK)
+        qf = []
+        for t in range(PACK):
+            turned = ps.tile([P, P], F32, name=f"turned{t}", tag=f"bank{t}")
+            nc.tensor.transpose(turned[:], dealt[:, t, :], ident[:])
+            terms = sb.tile([P, P], F32, name=f"terms{t}")
+            form = sb.tile([P, 1], F32, name=f"form{t}")
+            size = sb.tile([P, 1], F32, name=f"size{t}")
+            root = sb.tile([P, 1], F32, name=f"qf{t}")
+            nc.vector.scalar_tensor_tensor(terms[:], turned[:], 1.0, z_sb[last][:, t * P : (t + 1) * P], ALU.mult, ALU.mult, accum_out=form[:])
+            nc.scalar.activation(size[:], form[:], ACT.Abs, bias=part[:, t : t + 1])
+            nc.scalar.activation(root[:], size[:], ACT.Sqrt, bias=0.01, scale=1.0 / D)
+            qf.append(root)
+
+        y = sb.tile([P, PACK, Q], F32, name="y")
+        out_rows = out_0.rearrange("(p t) q -> p t q", t=PACK)
+        for t in range(PACK):
+            nc.vector.scalar_tensor_tensor(y[:, t, :], bold_sb[:], qf[t][:], a_ps[t // 2][:, t % 2, :], ALU.mult, ALU.add)
+            if t % 2 == 1:
+                nc.sync.dma_start(out_rows[:, t - 1 : t + 1, :], y[:, t - 1 : t + 1, :])
+
+        yw = sb.tile([P, Q], U32, name="yw", align_bytes=64)
+        ysc = sb.tile([P, Q], U8, name="ysc", align_bytes=64)
+        y_bf = [sb.tile([P, P, PACK], BF16, name=f"y_bf{h}", align_bytes=64) for h in range(2)]
+        for h in range(2):
+            interleave(nc.vector.tensor_copy if h == 0 else nc.scalar.copy, y_bf[h][:], y[:, :, h * P : (h + 1) * P])
+        for h in range(2):
+            nc.vector.quantize_mx(yw[:, h * P : (h + 1) * P].bitcast(FP8X4), ysc[:, h * P : (h + 1) * P], y_bf[h][:].rearrange("p n j -> p (n j)"))
+        nc.sync.dma_start(out_1[0].rearrange("p c r -> p (c r)").bitcast(I32), yw[:].bitcast(I32))
+        for g in range(4):
+            queue = nc.scalar if g < 2 else nc.sync
+            queue.dma_start(out_2[0, 4 * g : 4 * g + 4, :].bitcast(I32), ysc[32 * g : 32 * g + 4, :].bitcast(I32))

@@ -9,7 +9,6 @@ FLOPS = 2 * D * I * (K + Q)
 P = 128
 PACK = 4
 SHARE = 288
-SHARE_FUSED = 256
 F32 = mybir.dt.float32
 BF16 = mybir.dt.bfloat16
 I32 = mybir.dt.int32
@@ -40,21 +39,23 @@ def tile_attend_confidencebounds_pl_kernel(tc, cand_words, cand_scales, theta, i
         inv_raw = sb.tile([P, PACK, K], F32, name="inv_raw")
         theta_raw = sb.tile([P, PACK, Q], F32, name="theta_raw")
         bold_col = sb.tile([P, 2], F32, name="bold_col")
-        crow_sb = [sb.tile([P, T], F32, name=f"crow{c}") for c in range(chunks)]
+        crow_sb = [sb.tile([P, T], F32, name=f"crow{c}", tag=f"crow{c}") for c in range(chunks)]
         ident = sb.tile([P, P], F32, name="ident")
 
-        nc.vector.memset(scales[:].bitcast(I32), 0)
-        nc.sync.dma_start(offsets[:], offs)
+        nc.gpsimd.memset(scales[:].bitcast(I32), 0)
         nc.sync.dma_start(words[:].bitcast(I32), cand_words[0].bitcast(I32))
+        nc.sync.dma_start(offsets[:], offs)
         for g in range(4):
-            nc.scalar.dma_start(scales[32 * g : 32 * g + 4, :].bitcast(I32), cand_scales[0, 4 * g : 4 * g + 4, :].bitcast(I32))
+            nc.sync.dma_start(scales[32 * g : 32 * g + 4, :].bitcast(I32), cand_scales[0, 4 * g : 4 * g + 4, :].bitcast(I32))
         nc.sync.dma_start(inv_raw[:], inv.rearrange("(p j) k -> p j k", j=PACK))
-        nc.scalar.dma_start(bold_col[:], bold.rearrange("o (p j) -> p (o j)", j=2))
         for c in range(last):
             nc.sync.dma_start(crow_sb[c][:], crow[c * P : (c + 1) * P, :])
+        nc.sync.dma_start(bold_col[:], bold.rearrange("o (p j) -> p (o j)", j=2))
         nc.sync.dma_start(theta_raw[:], theta.rearrange("(p j) q -> p j q", j=PACK))
         nc.sync.dma_start(crow_sb[last][:], crow[last * P :, :])
         make_identity(nc, ident[:])
+        warm = sb.tile([P, 1], F32, name="warm")
+        nc.scalar.activation(warm[:], ident[:, 0:1], ACT.Sqrt, bias=0.01, scale=1.0 / D)
 
         cw = sb.tile([P, I], U16, name="cw", align_bytes=64)
         cs = sb.tile([P, I], U8, name="cs", align_bytes=64)
@@ -89,21 +90,20 @@ def tile_attend_confidencebounds_pl_kernel(tc, cand_words, cand_scales, theta, i
                 nc.vector.tensor_copy(ds[:], cs[:].rearrange("p (s t) -> p t s", t=PACK))
                 for t in range(PACK):
                     nc.tensor.matmul_mx(z_ps[:, t * P : (t + 1) * P], lhsT=dw[:, t, :].bitcast(FP4X4), lhsT_scale=ds[:, t, :], rhs=iw[:].bitcast(FP8X4), rhs_scale=isc[:], start=True, stop=True)
-            z = sb.tile([P, I], F32, name=f"z_sb{c}")
-            nc.scalar.copy(z[:], z_ps[:])
-            z_sb.append(z)
+            z_sb.append(z_ps)
+        z_last = sb.tile([P, I], F32, name="z_last")
+        nc.scalar.copy(z_last[:], z_sb[last][:])
+
+        def gather(c):
+            picked = sb.tile([P, I], F32, name=f"picked{c}")
+            nc.vector.tensor_copy(picked[:, :SHARE], crow_sb[c][:].indirect(offsets[:, : SHARE // 16]))
+            nc.scalar.activation(picked[:, SHARE:], crow_sb[c][:].indirect(offsets[:, SHARE // 16 :]), ACT.Copy)
+            return picked
 
         acc = ps.tile([P, PACK, P], F32, name="acc")
         for c in range(last):
             prod = sb.tile([P, I], F32, name=f"prod{c}")
-            if c < last - 1 or SHARE_FUSED == I:
-                nc.vector.tensor_tensor(prod[:], crow_sb[c][:].indirect(offsets[:]), z_sb[c][:], ALU.mult)
-            else:
-                n = SHARE_FUSED
-                rest = sb.tile([P, I - n], F32, name="rest")
-                nc.scalar.activation(rest[:], crow_sb[c][:].indirect(offsets[:, n // 16 :]), ACT.Copy)
-                nc.vector.tensor_tensor(prod[:, :n], crow_sb[c][:].indirect(offsets[:, : n // 16]), z_sb[c][:, :n], ALU.mult)
-                nc.vector.tensor_tensor(prod[:, n:], rest[:], z_sb[c][:, n:], ALU.mult)
+            nc.vector.tensor_tensor(prod[:], gather(c)[:], z_sb[c][:], ALU.mult)
             dealt = prod[:].rearrange("p (s t) -> p t s", t=PACK)
             for t in range(PACK):
                 nc.tensor.matmul(acc[:, t, :], lhsT=dealt[:, t, :], rhs=ident[:], is_transpose=True, start=(c == 0 and t == 0), stop=(c == last - 1 and t == PACK - 1))
@@ -117,10 +117,8 @@ def tile_attend_confidencebounds_pl_kernel(tc, cand_words, cand_scales, theta, i
         for t in range(PACK):
             nc.tensor.matmul_mx(a_ps[t // 2][:, t % 2, :], lhsT=dw[:, t, :].bitcast(FP4X4), lhsT_scale=ds[:, t, :], rhs=tw[:].bitcast(FP8X4), rhs_scale=tsc[:], start=True, stop=True)
 
-        picked = sb.tile([P, I], F32, name="picked")
-        nc.vector.tensor_copy(picked[:, :SHARE], crow_sb[last][:].indirect(offsets[:, : SHARE // 16]))
-        nc.scalar.activation(picked[:, SHARE:], crow_sb[last][:].indirect(offsets[:, SHARE // 16 :]), ACT.Copy)
-        part = sb.tile([P, PACK], F32, name="part")
+        picked = gather(last)
+        part = sb.tile([P, PACK], F32, name="part", tag=f"crow{last}")
         nc.vector.tensor_reduce(part[:], acc[:], mybir.AxisListType.X, ALU.add)
         dealt = picked[:].rearrange("p (s t) -> p t s", t=PACK)
         qf = []
@@ -131,7 +129,7 @@ def tile_attend_confidencebounds_pl_kernel(tc, cand_words, cand_scales, theta, i
             form = sb.tile([P, 1], F32, name=f"form{t}")
             size = sb.tile([P, 1], F32, name=f"size{t}")
             root = sb.tile([P, 1], F32, name=f"qf{t}")
-            nc.vector.scalar_tensor_tensor(terms[:], turned[:], 1.0, z_sb[last][:, t * P : (t + 1) * P], ALU.mult, ALU.mult, accum_out=form[:])
+            nc.vector.scalar_tensor_tensor(terms[:], turned[:], 1.0, z_last[:, t * P : (t + 1) * P], ALU.mult, ALU.mult, accum_out=form[:])
             nc.scalar.activation(size[:], form[:], ACT.Abs, bias=part[:, t : t + 1])
             nc.scalar.activation(root[:], size[:], ACT.Sqrt, bias=0.01, scale=1.0 / D)
             qf.append(root)

@@ -46,7 +46,7 @@ def tile_attend_confidencebounds_pl_kernel(tc, cand_words, cand_scales, theta, i
         nc.sync.dma_start(words[:].bitcast(I32), cand_words[0].bitcast(I32))
         nc.sync.dma_start(offsets[:], offs)
         for g in range(4):
-            nc.sync.dma_start(scales[32 * g : 32 * g + 4, :].bitcast(I32), cand_scales[0, 4 * g : 4 * g + 4, :].bitcast(I32))
+            nc.sync.dma_start(scales[g:P:32, :].bitcast(I32), cand_scales[0, g:16:4, :].bitcast(I32))
         nc.sync.dma_start(inv_raw[:], inv.rearrange("(p j) k -> p j k", j=PACK))
         for c in range(last):
             nc.sync.dma_start(crow_sb[c][:], crow[c * P : (c + 1) * P, :])
@@ -109,7 +109,8 @@ def tile_attend_confidencebounds_pl_kernel(tc, cand_words, cand_scales, theta, i
                 nc.tensor.matmul(acc[:, t, :], lhsT=dealt[:, t, :], rhs=ident[:], is_transpose=True, start=(c == 0 and t == 0), stop=(c == last - 1 and t == PACK - 1))
 
         theta_bf = sb.tile([P, Q, PACK], BF16, name="theta_bf", align_bytes=64)
-        interleave(nc.scalar.copy, theta_bf[:], theta_raw[:])
+        interleave(nc.vector.tensor_copy, theta_bf[:, :160, :], theta_raw[:, :, :160])
+        interleave(nc.scalar.copy, theta_bf[:, 160:, :], theta_raw[:, :, 160:])
         tw = sb.tile([P, Q], U32, name="theta_w", align_bytes=64)
         tsc = sb.tile([P, Q], U8, name="theta_s", align_bytes=64)
         nc.vector.quantize_mx(tw[:].bitcast(FP8X4), tsc[:], theta_bf[:].rearrange("p n j -> p (n j)"))
@@ -136,17 +137,20 @@ def tile_attend_confidencebounds_pl_kernel(tc, cand_words, cand_scales, theta, i
 
         y = sb.tile([P, PACK, Q], F32, name="y")
         out_rows = out_0.rearrange("(p t) q -> p t q", t=PACK)
-        for t in range(PACK):
-            nc.vector.scalar_tensor_tensor(y[:, t, :], bold_sb[:], qf[t][:], a_ps[t // 2][:, t % 2, :], ALU.mult, ALU.add)
-            if t % 2 == 1:
-                nc.sync.dma_start(out_rows[:, t - 1 : t + 1, :], y[:, t - 1 : t + 1, :])
+        for t in (0, 1):
+            nc.vector.scalar_tensor_tensor(y[:, t, :], bold_sb[:], qf[t][:], a_ps[0][:, t, :], ALU.mult, ALU.add)
+        nc.sync.dma_start(out_rows[:, 0:2, :], y[:, 0:2, :])
+        for cols in (slice(P, Q), slice(0, P)):
+            for t in (2, 3):
+                nc.vector.scalar_tensor_tensor(y[:, t, cols], bold_sb[:, cols], qf[t][:], a_ps[1][:, t - 2, cols], ALU.mult, ALU.add)
+        nc.sync.dma_start(out_rows[:, 2:4, :], y[:, 2:4, :])
 
         yw = sb.tile([P, Q], U32, name="yw", align_bytes=64)
         ysc = sb.tile([P, Q], U8, name="ysc", align_bytes=64)
         y_bf = [sb.tile([P, P, PACK], BF16, name=f"y_bf{h}", align_bytes=64) for h in range(2)]
         for h in range(2):
             interleave(nc.vector.tensor_copy if h == 0 else nc.scalar.copy, y_bf[h][:], y[:, :, h * P : (h + 1) * P])
-        for h in range(2):
+        for h in (1, 0):
             nc.vector.quantize_mx(yw[:, h * P : (h + 1) * P].bitcast(FP8X4), ysc[:, h * P : (h + 1) * P], y_bf[h][:].rearrange("p n j -> p (n j)"))
         nc.sync.dma_start(out_1[0].rearrange("p c r -> p (c r)").bitcast(I32), yw[:].bitcast(I32))
         for g in range(4):

from contextlib import ExitStack

import concourse.mybir as mybir
from concourse.masks import make_identity

D, K, T, I, Q = 512, 512, 2048, 512, 256
FLOPS = 2 * D * I * (K + Q)

P = 128
PACK = 4
SHARE = 288
F32 = mybir.dt.float32
BF16 = mybir.dt.bfloat16
I32 = mybir.dt.int32
U32 = mybir.dt.uint32
U16 = mybir.dt.uint16
U8 = mybir.dt.uint8
FP8X4 = mybir.dt.float8_e4m3fn_x4
FP4X4 = mybir.dt.float4_e2m1fn_x4
ALU = mybir.AluOpType
ACT = mybir.ActivationFunctionType


def interleave(copy, dst, src):
    copy(dst.rearrange("p (c i) j -> p c j i", i=4), src.rearrange("p j (c i) -> p c j i", i=4))


def tile_attend_confidencebounds_pl_kernel(tc, cand_words, cand_scales, theta, inv, crow, bold, offs, out_0, out_1, out_2):
    nc = tc.nc
    chunks = K // P
    last = chunks - 1
    with ExitStack() as ctx:
        sb = ctx.enter_context(tc.tile_pool(name="sb", bufs=1))
        ps = ctx.enter_context(tc.psum_pool(name="ps", bufs=1))

        offsets = sb.tile([P, I // 16], U16, name="offsets")
        words = sb.tile([P, T], U16, name="words", align_bytes=64)
        scales = sb.tile([P, T], U8, name="scales", align_bytes=64)
        inv_raw = sb.tile([P, PACK, K], F32, name="inv_raw")
        theta_raw = sb.tile([P, PACK, Q], F32, name="theta_raw")
        bold_col = sb.tile([P, 2], F32, name="bold_col")
        crow_sb = [sb.tile([P, T], F32, name=f"crow{c}", tag=f"crow{c}") for c in range(chunks)]
        ident = sb.tile([P, P], F32, name="ident")

        nc.gpsimd.memset(scales[:].bitcast(I32), 0)
        nc.sync.dma_start(words[:].bitcast(I32), cand_words[0].bitcast(I32))
        nc.sync.dma_start(offsets[:], offs)
        for g in range(4):
            nc.sync.dma_start(scales[g:P:32, :].bitcast(I32), cand_scales[0, g:16:4, :].bitcast(I32))
        nc.sync.dma_start(inv_raw[:], inv.rearrange("(p j) k -> p j k", j=PACK))
        for c in range(last):
            nc.sync.dma_start(crow_sb[c][:], crow[c * P : (c + 1) * P, :])
        nc.sync.dma_start(bold_col[:], bold.rearrange("o (p j) -> p (o j)", j=2))
        nc.sync.dma_start(theta_raw[:], theta.rearrange("(p j) q -> p j q", j=PACK))
        nc.sync.dma_start(crow_sb[last][:], crow[last * P :, :])
        make_identity(nc, ident[:])
        warm = sb.tile([P, 1], F32, name="warm")
        nc.scalar.activation(warm[:], ident[:, 0:1], ACT.Sqrt, bias=0.01, scale=1.0 / D)

        cw = sb.tile([P, I], U16, name="cw", align_bytes=64)
        cs = sb.tile([P, I], U8, name="cs", align_bytes=64)
        nc.vector.tensor_copy(cw[:], words[:].indirect(offsets[:]))
        nc.vector.tensor_copy(cs[:], scales[:].indirect(offsets[:]))

        bold_ps = ps.tile([P, 512], F32, name="bold_ps", tag="spare")
        for j in range(2):
            nc.tensor.transpose(bold_ps[:, j * P : (j + 1) * P], bold_col[:, j : j + 1].to_broadcast([P, P]), ident[:])
        bold_sb = sb.tile([P, Q], F32, name="bold_sb")
        nc.scalar.copy(bold_sb[:].rearrange("p (n j) -> p n j", j=2), bold_ps[:, 0:Q].rearrange("p (j n) -> p n j", j=2))

        inv_bf = []
        for c in range(chunks):
            b = sb.tile([P, P, PACK], BF16, name=f"inv_bf{c}", align_bytes=64)
            interleave(nc.vector.tensor_copy if c < 2 else nc.scalar.copy, b[:], inv_raw[:, :, c * P : (c + 1) * P])
            inv_bf.append(b)

        dw = sb.tile([P, PACK, P], U16, name="dw", align_bytes=64)
        ds = sb.tile([P, PACK, P], U8, name="ds", align_bytes=64)

        z_sb = []
        for c in range(chunks):
            iw = sb.tile([P, P], U32, name=f"inv_w{c}", align_bytes=64)
            isc = sb.tile([P, P], U8, name=f"inv_s{c}", align_bytes=64)
            nc.vector.quantize_mx(iw[:].bitcast(FP8X4), isc[:], inv_bf[c][:].rearrange("p n j -> p (n j)"))
            z_ps = ps.tile([P, I], F32, name=f"z_ps{c}", tag=f"bank{c}")
            if c < last:
                nc.tensor.matmul_mx(z_ps[:], lhsT=iw[:].bitcast(FP8X4), lhsT_scale=isc[:], rhs=cw[:].bitcast(FP4X4), rhs_scale=cs[:], start=True, stop=True)
            else:
                nc.vector.tensor_copy(dw[:], cw[:].rearrange("p (s t) -> p t s", t=PACK))
                nc.vector.tensor_copy(ds[:], cs[:].rearrange("p (s t) -> p t s", t=PACK))
                for t in range(PACK):
                    nc.tensor.matmul_mx(z_ps[:, t * P : (t + 1) * P], lhsT=dw[:, t, :].bitcast(FP4X4), lhsT_scale=ds[:, t, :], rhs=iw[:].bitcast(FP8X4), rhs_scale=isc[:], start=True, stop=True)
            z_sb.append(z_ps)
        z_last = sb.tile([P, I], F32, name="z_last")
        nc.scalar.copy(z_last[:], z_sb[last][:])

        def gather(c):
            picked = sb.tile([P, I], F32, name=f"picked{c}")
            nc.vector.tensor_copy(picked[:, :SHARE], crow_sb[c][:].indirect(offsets[:, : SHARE // 16]))
            nc.scalar.activation(picked[:, SHARE:], crow_sb[c][:].indirect(offsets[:, SHARE // 16 :]), ACT.Copy)
            return picked

        acc = ps.tile([P, PACK, P], F32, name="acc")
        for c in range(last):
            prod = sb.tile([P, I], F32, name=f"prod{c}")
            nc.vector.tensor_tensor(prod[:], gather(c)[:], z_sb[c][:], ALU.mult)
            dealt = prod[:].rearrange("p (s t) -> p t s", t=PACK)
            for t in range(PACK):
                nc.tensor.matmul(acc[:, t, :], lhsT=dealt[:, t, :], rhs=ident[:], is_transpose=True, start=(c == 0 and t == 0), stop=(c == last - 1 and t == PACK - 1))

        theta_bf = sb.tile([P, Q, PACK], BF16, name="theta_bf", align_bytes=64)
        interleave(nc.vector.tensor_copy, theta_bf[:, :160, :], theta_raw[:, :, :160])
        interleave(nc.scalar.copy, theta_bf[:, 160:, :], theta_raw[:, :, 160:])
        tw = sb.tile([P, Q], U32, name="theta_w", align_bytes=64)
        tsc = sb.tile([P, Q], U8, name="theta_s", align_bytes=64)
        nc.vector.quantize_mx(tw[:].bitcast(FP8X4), tsc[:], theta_bf[:].rearrange("p n j -> p (n j)"))
        a_ps = [ps.tile([P, 2, Q], F32, name=f"a_ps{h}") for h in range(2)]
        for t in range(PACK):
            nc.tensor.matmul_mx(a_ps[t // 2][:, t % 2, :], lhsT=dw[:, t, :].bitcast(FP4X4), lhsT_scale=ds[:, t, :], rhs=tw[:].bitcast(FP8X4), rhs_scale=tsc[:], start=True, stop=True)

        picked = gather(last)
        part = sb.tile([P, PACK], F32, name="part", tag=f"crow{last}")
        nc.vector.tensor_reduce(part[:], acc[:], mybir.AxisListType.X, ALU.add)
        dealt = picked[:].rearrange("p (s t) -> p t s", t=PACK)
        qf = []
        for t in range(PACK):
            turned = ps.tile([P, P], F32, name=f"turned{t}", tag=f"bank{t}")
            nc.tensor.transpose(turned[:], dealt[:, t, :], ident[:])
            terms = sb.tile([P, P], F32, name=f"terms{t}")
            form = sb.tile([P, 1], F32, name=f"form{t}")
            size = sb.tile([P, 1], F32, name=f"size{t}")
            root = sb.tile([P, 1], F32, name=f"qf{t}")
            nc.vector.scalar_tensor_tensor(terms[:], turned[:], 1.0, z_last[:, t * P : (t + 1) * P], ALU.mult, ALU.mult, accum_out=form[:])
            nc.scalar.activation(size[:], form[:], ACT.Abs, bias=part[:, t : t + 1])
            nc.scalar.activation(root[:], size[:], ACT.Sqrt, bias=0.01, scale=1.0 / D)
            qf.append(root)

        y = sb.tile([P, PACK, Q], F32, name="y")
        out_rows = out_0.rearrange("(p t) q -> p t q", t=PACK)
        for t in (0, 1):
            nc.vector.scalar_tensor_tensor(y[:, t, :], bold_sb[:], qf[t][:], a_ps[0][:, t, :], ALU.mult, ALU.add)
        nc.sync.dma_start(out_rows[:, 0:2, :], y[:, 0:2, :])
        for cols in (slice(P, Q), slice(0, P)):
            for t in (2, 3):
                nc.vector.scalar_tensor_tensor(y[:, t, cols], bold_sb[:, cols], qf[t][:], a_ps[1][:, t - 2, cols], ALU.mult, ALU.add)
        nc.sync.dma_start(out_rows[:, 2:4, :], y[:, 2:4, :])

        yw = sb.tile([P, Q], U32, name="yw", align_bytes=64)
        ysc = sb.tile([P, Q], U8, name="ysc", align_bytes=64)
        y_bf = [sb.tile([P, P, PACK], BF16, name=f"y_bf{h}", align_bytes=64) for h in range(2)]
        for h in range(2):
            interleave(nc.vector.tensor_copy if h == 0 else nc.scalar.copy, y_bf[h][:], y[:, :, h * P : (h + 1) * P])
        for h in (1, 0):
            nc.vector.quantize_mx(yw[:, h * P : (h + 1) * P].bitcast(FP8X4), ysc[:, h * P : (h + 1) * P], y_bf[h][:].rearrange("p n j -> p (n j)"))
        nc.sync.dma_start(out_1[0].rearrange("p c r -> p (c r)").bitcast(I32), yw[:].bitcast(I32))
        for g in range(4):
            queue = nc.scalar if g < 2 else nc.sync
            queue.dma_start(out_2[0, 4 * g : 4 * g + 4, :].bitcast(I32), ysc[32 * g : 32 * g + 4, :].bitcast(I32))
